import numpy as np
import ml_dtypes


def mxq(x, axis, fmt="e4m3"):
    dtype, down = {"e4m3": (ml_dtypes.float8_e4m3fn, 7), "e5m2": (ml_dtypes.float8_e5m2, 14)}[fmt]
    v = np.moveaxis(np.asarray(x, np.float32).astype(ml_dtypes.bfloat16).astype(np.float64), axis, -1)
    blocks = v.reshape(v.shape[:-1] + (-1, 32))
    amax = np.abs(blocks).max(-1, keepdims=True)
    byte = np.maximum(np.where(amax > 0, np.frexp(amax)[1] - 1 + 127, 0) - down, 1)
    scale = np.exp2(byte - 127.0)
    codes = (blocks / scale).astype(np.float32).astype(dtype).astype(np.float64)
    return np.moveaxis((codes * scale).reshape(v.shape), -1, axis)


WIDE = False


def mx_kscale(k):
    if not WIDE:
        return np.ones(k)
    levels = np.array([10, -10, 5, -5, 0])
    if k % 512:
        return np.exp2(np.random.permutation(np.resize(levels, k // 32))).repeat(32)
    a = np.empty((k // 512, 16))
    for p in range(k // 512):
        a[p, :8] = np.random.permutation(np.resize(levels, 8))
        for g in range(8):
            far = levels[np.abs(levels - a[p, g]) >= 10]
            a[p, g + 8] = far[np.random.randint(len(far))]
    return np.exp2(a.ravel()).repeat(32)


def f64(x):
    return np.asarray(x).astype(np.float64)


def striped(idx):
    return np.tile(idx.reshape(-1, 16).T, (8, 1)).astype(np.uint16)


def unstriped(offs):
    return offs[:16].T.reshape(-1).astype(np.int64)


E2M1 = np.array([0.0, 0.5, 1.0, 1.5, 2.0, 3.0, 4.0, 6.0, -0.0, -0.5, -1.0, -1.5, -2.0, -3.0, -4.0, -6.0])


def pack_weight(w, fmt):
    k, n = w.shape
    w = f64(np.asarray(w, np.float32).astype(ml_dtypes.bfloat16)).reshape(k // 32, 32, n)
    amax = np.abs(w).max(1)
    if fmt == "e4m3":
        byte = np.frexp(amax)[1] - 1 + 127 - 7
    else:
        mant, ex = np.frexp(amax / 6.0)
        byte = np.where(mant > 0.5, ex, ex - 1) + 127
    byte = np.clip(np.where(amax > 0, byte, 1), 1, 254)
    scaled = (w * np.exp2(127.0 - byte)[:, None, :]).reshape(k, n).astype(np.float32)
    by_word = np.ascontiguousarray(scaled.reshape(k // 512, 128, 4, n).transpose(0, 1, 3, 2))
    if fmt == "e4m3":
        words = by_word.astype(ml_dtypes.float8_e4m3fn).view(np.uint8)
    else:
        c = by_word.astype(ml_dtypes.float4_e2m1fn).view(np.uint8) & 0xF
        words = (c[..., 0::2] | (c[..., 1::2] << 4)).reshape(k // 512, 128, 2 * n)
    return np.ascontiguousarray(words), np.ascontiguousarray(byte.astype(np.uint8).reshape(k // 512, 16, n))


def unpack_weight(words, scales, fmt):
    g, _, n = scales.shape
    words = np.ascontiguousarray(words).reshape(g, 128, n, -1)
    if fmt == "e4m3":
        vals = words.view(ml_dtypes.float8_e4m3fn).astype(np.float64)
    else:
        nib = np.empty((g, 128, n, 4), np.uint8)
        nib[..., 0::2] = words & 0xF
        nib[..., 1::2] = words >> 4
        vals = E2M1[nib]
    vals = vals * np.repeat(np.exp2(scales.astype(np.float64) - 127.0), 8, axis=1)[..., None]
    return vals.transpose(0, 1, 3, 2).reshape(g * 512, n)


def gelu(v):
    return 0.5 * v * (1.0 + np.tanh(np.sqrt(2.0 / np.pi) * (v + 0.044715 * v**3)))


def often(T, S):
    return np.random.permutation(T)[(T * np.random.uniform(0, 1, S) ** 4).astype(np.int64)]


def bf(x):
    return np.asarray(x, np.float32).astype(ml_dtypes.bfloat16)


def planes(Y):
    n, m = Y.shape
    b = f64(bf(Y)).reshape(n // 32, 32, m)
    amax = np.abs(b).max(1)
    byte = np.clip(np.where(amax > 0, np.frexp(amax)[1] - 1 + 127 - 7, 1), 1, 254)
    codes = (b * np.exp2(127.0 - byte)[:, None, :]).reshape(n, m).astype(np.float32).astype(ml_dtypes.float8_e4m3fn).view(np.uint8)
    words = codes.reshape(n // 512, 128, 4, m).transpose(0, 1, 3, 2)
    return np.ascontiguousarray(words), np.ascontiguousarray(byte.astype(np.uint8).reshape(n // 512, 16, m))


K, K2, T, S, P, H, N = 1024, 512, 2048, 1024, 512, 1024, 1024


def setup_inputs():
    n = np.random.standard_normal
    s = mx_kscale(K)[:, None]
    s2 = mx_kscale(K2)[:, None]
    u = mx_kscale(H)[:, None]
    x = {}
    x["tab_words"], x["tab_scales"] = pack_weight(n((K, T)) * s, "e4m3")
    x["tab2_words"], x["tab2_scales"] = pack_weight(n((K2, T)) * s2, "e4m3")
    x["tab3_words"], x["tab3_scales"] = pack_weight(n((K2, T)) * s2, "e4m3")
    x["offs"] = striped(np.random.permutation(T)[:S])
    x["offs2"] = striped(np.random.permutation(T)[:S])
    x["offs3"] = striped(np.random.permutation(T)[:S])
    x["pos1"] = striped(np.random.permutation(S)[:P])
    x["pos2"] = striped(often(S, P))
    x["pos3"] = striped(often(S, P))
    x["w1"] = (n((K, H)) / K**0.5 / s).astype(np.float32)
    x["w2_words"], x["w2_scales"] = pack_weight(n((K2, H)) / K2**0.5 / s2, "e2m1")
    x["w3_words"], x["w3_scales"] = pack_weight(n((K2, H)) / K2**0.5 / s2 * u.T, "e4m3")
    x["margin"] = (0.7 * n(H)).astype(np.float32)
    x["w4"] = (n((H, N)) / H**0.5 / u * np.exp(0.8 * n(N))).astype(np.float32)
    x["keep"] = np.exp(0.5 * n((N, P))).astype(np.float32)
    return x


def reference(tab_words, tab_scales, tab2_words, tab2_scales, tab3_words, tab3_scales, offs, offs2, offs3,
              pos1, pos2, pos3, w1, w2_words, w2_scales, w3_words, w3_scales, margin, w4, keep):
    v = unpack_weight(tab_words, tab_scales, "e4m3")[:, unstriped(offs)]
    v2 = unpack_weight(tab2_words, tab2_scales, "e4m3")[:, unstriped(offs2)]
    v3 = unpack_weight(tab3_words, tab3_scales, "e4m3")[:, unstriped(offs3)]
    a = mxq(f64(w1), 0, "e4m3").T @ v
    b = unpack_weight(w2_words, w2_scales, "e2m1").T @ v2
    d = unpack_weight(w3_words, w3_scales, "e4m3").T @ v3
    low = np.minimum(a[:, unstriped(pos1)] + f64(margin)[:, None], b[:, unstriped(pos2)])
    z = low * d[:, unstriped(pos3)]
    y = (mxq(f64(w4), 0, "e4m3").T @ mxq(z, 0, "e4m3")) * f64(keep)
    words, scales = planes(y)
    return y, words, scales

@@ -1,0 +1,289 @@
+from contextlib import ExitStack
+
+import concourse.mybir as mybir
+
+K, K2, T, S, J, H, N = 1024, 512, 2048, 1024, 512, 1024, 1024
+FLOPS = 2 * S * H * (K + 2 * K2) + 2 * J * H * N
+
+F32 = mybir.dt.float32
+BF16 = mybir.dt.bfloat16
+I32 = mybir.dt.int32
+U32 = mybir.dt.uint32
+U16 = mybir.dt.uint16
+U8 = mybir.dt.uint8
+FP8X4 = mybir.dt.float8_e4m3fn_x4
+FP4X4 = mybir.dt.float4_e2m1fn_x4
+ALU = mybir.AluOpType
+
+P = 128
+PACK = 4
+PASS = P * PACK
+BANK = 512
+QUADS = 4
+
+
+def tile_list_zoo_transfer_join_kernel(
+    tc, tab_words, tab_scales, tab2_words, tab2_scales, tab3_words, tab3_scales, offs, offs2, offs3,
+    pos1, pos2, pos3, w1, w2_words, w2_scales, w3_words, w3_scales, margin, w4, keep, out_0, out_1, out_2,
+):
+    nc = tc.nc
+    with ExitStack() as ctx:
+        lists = ctx.enter_context(tc.tile_pool(name="lists", bufs=1))
+        held = ctx.enter_context(tc.tile_pool(name="held", bufs=1))
+        shared = ctx.enter_context(tc.tile_pool(name="shared", bufs=1))
+        rounded = ctx.enter_context(tc.tile_pool(name="rounded", bufs=4))
+        picks = ctx.enter_context(tc.tile_pool(name="picks", bufs=2))
+        psum = ctx.enter_context(tc.psum_pool(name="psum", bufs=1))
+
+        banks = [psum.tile([P, BANK], F32, name="bank%d" % i) for i in range(8)]
+
+        def load_list(src, name):
+            tile = lists.tile([P, src.shape[1]], U16, name=name)
+            nc.sync.dma_start(tile[:], src)
+            return tile
+
+        def load_words(src, name, slot):
+            tile = shared.tile([P, T], I32, name=name, tag=slot, align_bytes=64)
+            nc.sync.dma_start(tile[:], src.rearrange("p n t -> p (n t)").bitcast(I32))
+            return tile
+
+        def load_scales(src, name, slot, zero_on):
+            passes, width = src.shape[0], src.shape[2]
+            tile = shared.tile([P, width], U8, name=name, tag=slot, align_bytes=64)
+            zero_on.memset(tile[:].bitcast(I32), 0)
+            for q in range(QUADS):
+                rows = src[:, 4 * q : 4 * q + 4, :] if passes > 1 else src[0, 4 * q : 4 * q + 4, :]
+                nc.scalar.dma_start(tile[32 * q : 32 * q + 4 * passes, :].bitcast(I32), rows.bitcast(I32))
+            return tile
+
+        def pick_words(window, offsets, name):
+            tile = held.tile([P, S], U32, name=name, align_bytes=64)
+            nc.vector.tensor_copy(tile[:], window.bitcast(U32).indirect(offsets[:]))
+            return tile
+
+        def pick_scales(window, offsets, name):
+            tile = held.tile([P, S], U8, name=name, align_bytes=64)
+            nc.vector.tensor_copy(tile[:], window[:].indirect(offsets[:]))
+            return tile
+
+        def deal(raw, name):
+            tile = held.tile([P, raw.shape[1]], U8, name=name, align_bytes=64)
+            nc.vector.tensor_copy(
+                tile[:].bitcast(I32).rearrange("p (g t u w) -> p g t u w", g=2, t=PACK, u=32),
+                raw[:].bitcast(I32).rearrange("p (g u t w) -> p g t u w", g=2, t=PACK, u=32),
+            )
+            return tile
+
+        def load_packed(src, name):
+            tile = held.tile([P, src.shape[1]], U8, name=name, align_bytes=64)
+            nc.sync.dma_start(tile[:].bitcast(I32), src.bitcast(I32))
+            return tile
+
+        idx2 = load_list(offs2, "idx2")
+        win2 = load_words(tab2_words[0], "win2", "B")
+        swin2 = load_scales(tab2_scales, "swin2", "C", nc.gpsimd)
+        w2_sraw = load_scales(w2_scales, "w2_sraw", "F", nc.vector)
+        idx3 = load_list(offs3, "idx3")
+        idx1 = load_list(offs, "idx1")
+        p2 = load_list(pos2, "p2")
+        p3 = load_list(pos3, "p3")
+        p1 = load_list(pos1, "p1")
+        w2_raw = load_packed(w2_words[0], "w2_raw")
+        swin3 = load_scales(tab3_scales, "swin3", "D", nc.vector)
+        w3_sraw = load_scales(w3_scales, "w3_sraw", "G", nc.vector)
+        swin1 = load_scales(tab_scales, "swin1", "E", nc.vector)
+
+        def load_margin(i):
+            g, t = divmod(i, PACK)
+            col = held.tile([P, 1], F32, name="margin%d" % i)
+            dealt = margin[PASS * g : PASS * (g + 1)].rearrange("(u t e o) -> t u e o", t=PACK, e=4, o=1)
+            with nc.allow_non_contiguous_dma(reason="one margin value a partition"):
+                nc.gpsimd.dma_start(col[:], dealt[t])
+            return col
+
+        def load_w1(g, slot):
+            raw = shared.tile([P, 2, PACK, PASS], F32, name="w1_raw%d" % g, tag=slot, align_bytes=64)
+            for a in range(2):
+                nc.sync.dma_start(
+                    raw[:, a, :, :],
+                    w1[PASS * a : PASS * (a + 1), PASS * g : PASS * (g + 1)].rearrange("(p j) c -> p j c", j=PACK),
+                )
+            return raw
+
+        def load_keep(c, slot):
+            tile = shared.tile([P, PACK, J], F32, name="keep%d" % c, tag=slot, align_bytes=64)
+            nc.sync.dma_start(tile[:], keep[PASS * c : PASS * (c + 1), :].rearrange("(p t) j -> p t j", t=PACK))
+            return tile
+
+        def load_w4(g, slot):
+            raw = shared.tile([P, PACK, N], F32, name="w4_raw%d" % g, tag=slot, align_bytes=64)
+            rows = w4[PASS * g : PASS * (g + 1), :].rearrange("(u t e) n -> t u e n", t=PACK, e=4)
+            for t in range(PACK):
+                nc.sync.dma_start(raw[:, t, :], rows[t])
+            return raw
+
+        margins = [load_margin(i) for i in range(2 * PACK)]
+        w1_raw = [load_w1(0, "A")]
+        w3_raw = load_packed(w3_words[0].rearrange("p n t -> p (n t)"), "w3_raw")
+
+        v2 = pick_words(win2[:], idx2, "v2")
+        win3 = load_words(tab3_words[0], "win3", "B")
+        s2 = pick_scales(swin2, idx2, "s2")
+        win1 = shared.tile([P, 2, T], I32, name="win1", tag="C", align_bytes=64)
+        for a in range(2):
+            nc.sync.dma_start(win1[:, a, :], tab_words[a].rearrange("p n t -> p (n t)").bitcast(I32))
+        w2 = deal(w2_raw, "w2")
+        w2_s = deal(w2_sraw, "w2_s")
+        v3 = pick_words(win3[:], idx3, "v3")
+        w1_raw.append(load_w1(1, "B"))
+        s3 = pick_scales(swin3, idx3, "s3")
+        w4_raw = {1: load_w4(1, "D")}
+        w3 = deal(w3_raw, "w3")
+        w3_s = deal(w3_sraw, "w3_s")
+        s1 = pick_scales(swin1, idx1, "s1")
+        v1 = [pick_words(win1[:, a, :], idx1, "v1_%d" % a) for a in range(2)]
+        keeps = [load_keep(0, "G"), load_keep(1, "E")]
+
+        NB, NA = 4, 4
+        b_rows = [held.tile([P, S], F32, name="b_rows%d" % i) for i in range(NB)]
+        d_rows = [held.tile([P, S], F32, name="d_rows%d" % i) for i in range(NB)]
+        a_rows = [held.tile([P, S], F32, name="a_rows%d" % i) for i in range(NA)]
+        w1_q = [held.tile([P, 2, P], U32, name="w1_q%d" % i, align_bytes=64) for i in range(8)]
+        w1_s = [held.tile([P, 2, P], U8, name="w1_s%d" % i, align_bytes=64) for i in range(8)]
+
+        def quantize(codes, scales, stage):
+            nc.vector.quantize_mx(out=codes.bitcast(FP8X4), scales=scales, in_=stage)
+
+        def make_w1(i):
+            g, t = divmod(i, PACK)
+            stage = rounded.tile([P, 2 * PASS], BF16, name="w1_bf%d" % i, tag="w1_bf", align_bytes=64)
+            nc.scalar.copy(
+                stage[:].rearrange("p (a u e j) -> p a u j e", a=2, e=4, j=PACK),
+                w1_raw[g][:].rearrange("p a j (u t e) -> p t a u j e", t=PACK, e=4)[:, t],
+            )
+            quantize(w1_q[i][:].rearrange("p a m -> p (a m)"), w1_s[i][:].rearrange("p a m -> p (a m)"), stage[:])
+
+        def make_b(i):
+            for h in range(2):
+                cols = slice(BANK * h, BANK * (h + 1))
+                nc.tensor.matmul_mx(
+                    out=banks[h][:], lhsT=w2[:, 2 * P * i : 2 * P * (i + 1)].bitcast(FP4X4),
+                    lhsT_scale=w2_s[:, P * i : P * (i + 1)], rhs=v2[:, cols].bitcast(FP8X4), rhs_scale=s2[:, cols],
+                    start=True, stop=True,
+                )
+                nc.scalar.copy(b_rows[i % NB][:, cols], banks[h][:])
+
+        def make_d(i):
+            for h in range(2):
+                cols = slice(BANK * h, BANK * (h + 1))
+                nc.tensor.matmul_mx(
+                    out=banks[2 + h][:], lhsT=w3[:, 4 * P * i : 4 * P * (i + 1)].bitcast(FP8X4),
+                    lhsT_scale=w3_s[:, P * i : P * (i + 1)], rhs=v3[:, cols].bitcast(FP8X4), rhs_scale=s3[:, cols],
+                    start=True, stop=True,
+                )
+                nc.scalar.copy(d_rows[i % NB][:, cols], banks[2 + h][:])
+
+        def make_a(i):
+            for h in range(2):
+                cols = slice(BANK * h, BANK * (h + 1))
+                bank = banks[4 + 2 * (i % 2) + h]
+                for a in range(2):
+                    nc.tensor.matmul_mx(
+                        out=bank[:], lhsT=w1_q[i][:, a, :].bitcast(FP8X4), lhsT_scale=w1_s[i][:, a, :],
+                        rhs=v1[a][:, cols].bitcast(FP8X4), rhs_scale=s1[4 * a :, cols],
+                        start=(a == 0), stop=(a == 1),
+                    )
+                nc.scalar.copy(a_rows[i % NA][:, cols], bank[:])
+
+        low = held.tile([P, PACK, J], F32, name="low")
+        joined = shared.tile([P, 2, PACK, J], F32, name="joined", tag="C", align_bytes=64)
+        zoo, crate = joined[:, 0], joined[:, 1]
+        z_q = [held.tile([P, J], U32, name="z_q%d" % g, align_bytes=64) for g in range(2)]
+        z_s = [held.tile([P, J], U8, name="z_s%d" % g, align_bytes=64) for g in range(2)]
+        w4_q = [[held.tile([P, PASS], U32, name="w4_q%d%d" % (g, c), align_bytes=64) for c in range(2)] for g in range(2)]
+        w4_s = [[held.tile([P, PASS], U8, name="w4_s%d%d" % (g, c), align_bytes=64) for c in range(2)] for g in range(2)]
+
+        def join(i):
+            g, t = divmod(i, PACK)
+            animal = picks.tile([P, J], F32, name="animal%d" % i, tag="animal")
+            nc.vector.tensor_copy(zoo[:, t, :], b_rows[i % NB][:].indirect(p2[:]))
+            nc.vector.tensor_copy(animal[:], a_rows[i % NA][:].indirect(p1[:]))
+            nc.vector.tensor_copy(crate[:, t, :], d_rows[i % NB][:].indirect(p3[:]))
+            nc.vector.scalar_tensor_tensor(
+                out=low[:, t, :], in0=animal[:], scalar=margins[i][:], in1=zoo[:, t, :], op0=ALU.add, op1=ALU.min
+            )
+
+        def make_z(g):
+            stage = rounded.tile([P, J * PACK], BF16, name="z_bf%d" % g, tag="rounded", align_bytes=64)
+            nc.vector.tensor_tensor(
+                out=stage[:].rearrange("p (c i t) -> p c t i", i=4, t=PACK),
+                in0=low[:].rearrange("p t (c i) -> p c t i", i=4),
+                in1=crate.rearrange("p t (c i) -> p c t i", i=4),
+                op=ALU.mult,
+            )
+            quantize(z_q[g][:], z_s[g][:], stage[:])
+
+        def make_w4(g, c):
+            stage = rounded.tile([P, PASS * PACK], BF16, name="w4_bf%d%d" % (g, c), tag="rounded", align_bytes=64)
+            nc.scalar.copy(
+                stage[:].rearrange("p (t m j) -> p m j t", t=PACK, j=PACK),
+                w4_raw[g][:, :, PASS * c : PASS * (c + 1)].rearrange("p j (m t) -> p m j t", t=PACK),
+            )
+            quantize(w4_q[g][c][:], w4_s[g][c][:], stage[:])
+
+        AHEAD = 2
+        for i in range(AHEAD):
+            make_b(i)
+            make_d(i)
+        for i in range(PACK):
+            make_w1(i)
+        w4_raw[0] = load_w4(0, "A")
+        for i in range(AHEAD):
+            make_a(i)
+        for i in range(8):
+            ahead = i + AHEAD
+            if ahead < 8:
+                if ahead + AHEAD < 8:
+                    make_w1(ahead + AHEAD)
+                make_b(ahead)
+                make_d(ahead)
+                make_a(ahead)
+            if i >= 5:
+                make_w4(*divmod(i - 5, 2))
+            join(i)
+            if i % PACK == PACK - 1:
+                make_z(i // PACK)
+        make_w4(1, 1)
+
+        for g in range(2):
+            for i in range(8):
+                c, t = divmod(i, PACK)
+                cols = slice(P * t, P * (t + 1))
+                nc.tensor.matmul_mx(
+                    out=banks[i][:], lhsT=w4_q[g][c][:, cols].bitcast(FP8X4), lhsT_scale=w4_s[g][c][:, cols],
+                    rhs=z_q[g][:].bitcast(FP8X4), rhs_scale=z_s[g][:], start=(g == 0), stop=(g == 1),
+                )
+        y_s = held.tile([P, 2, J], U8, name="y_s", align_bytes=64)
+        for c in range(2):
+            y = shared.tile([P, PACK, J], F32, name="y%d" % c, tag="BA"[c], align_bytes=64)
+            rows = out_0[PASS * c : PASS * (c + 1), :].rearrange("(p t) j -> p t j", t=PACK)
+            for t in range(PACK):
+                nc.vector.tensor_tensor(out=y[:, t, :], in0=banks[PACK * c + t][:], in1=keeps[c][:, t, :], op=ALU.mult)
+                if t % 2 == 1:
+                    nc.sync.dma_start(rows[:, t - 1 : t + 1, :], y[:, t - 1 : t + 1, :])
+            stage = rounded.tile([P, J * PACK], BF16, name="y_bf%d" % c, tag="rounded", align_bytes=64)
+            dealt = stage[:].rearrange("p (c i t) -> p c t i", i=4, t=PACK)
+            source = y[:].rearrange("p t (c i) -> p c t i", i=4)
+            if c == 0:
+                nc.scalar.copy(dealt, source)
+            else:
+                nc.vector.tensor_copy(dealt, source)
+            y_q = held.tile([P, J], U32, name="y_q%d" % c, align_bytes=64)
+            quantize(y_q[:], y_s[:, c, :], stage[:])
+            nc.sync.dma_start(out_1[c].rearrange("p n t -> p (n t)").bitcast(I32), y_q[:].bitcast(I32))
+        for q in range(QUADS):
+            queue = nc.sync if q % 2 == 0 else nc.scalar
+            queue.dma_start(
+                out_2[:, 4 * q : 4 * q + 4, :].rearrange("g r j -> r g j").bitcast(I32),
+                y_s[32 * q : 32 * q + 4, :, :].bitcast(I32),
+            )

@@ -20,6 +20,7 @@ PACK = 4
 PASS = P * PACK
 BANK = 512
 QUADS = 4
+SCALAR_SHARE = 40
 
 
 def tile_list_zoo_transfer_join_kernel(
@@ -31,7 +32,7 @@ def tile_list_zoo_transfer_join_kernel(
         lists = ctx.enter_context(tc.tile_pool(name="lists", bufs=1))
         held = ctx.enter_context(tc.tile_pool(name="held", bufs=1))
         shared = ctx.enter_context(tc.tile_pool(name="shared", bufs=1))
-        rounded = ctx.enter_context(tc.tile_pool(name="rounded", bufs=4))
+        rounded = ctx.enter_context(tc.tile_pool(name="rounded", bufs=5))
         picks = ctx.enter_context(tc.tile_pool(name="picks", bufs=2))
         psum = ctx.enter_context(tc.psum_pool(name="psum", bufs=1))
 
@@ -47,17 +48,21 @@ def tile_list_zoo_transfer_join_kernel(
             nc.sync.dma_start(tile[:], src.rearrange("p n t -> p (n t)").bitcast(I32))
             return tile
 
-        def load_scales(src, name, slot, zero_on):
-            passes, width = src.shape[0], src.shape[2]
-            tile = shared.tile([P, width], U8, name=name, tag=slot, align_bytes=64)
+        def load_scales(sources, name, slot, zero_on):
+            tile = shared.tile([P, sources[0].shape[2]], U8, name=name, tag=slot, align_bytes=64)
             zero_on.memset(tile[:].bitcast(I32), 0)
-            for q in range(QUADS):
-                rows = src[:, 4 * q : 4 * q + 4, :] if passes > 1 else src[0, 4 * q : 4 * q + 4, :]
-                nc.scalar.dma_start(tile[32 * q : 32 * q + 4 * passes, :].bitcast(I32), rows.bitcast(I32))
+            first = 0
+            for src in sources:
+                passes = src.shape[0]
+                for q in range(QUADS):
+                    rows = src[:, 4 * q : 4 * q + 4, :] if passes > 1 else src[0, 4 * q : 4 * q + 4, :]
+                    start = 32 * q + first
+                    nc.scalar.dma_start(tile[start : start + 4 * passes, :].bitcast(I32), rows.bitcast(I32))
+                first += 4 * passes
             return tile
 
         def pick_words(window, offsets, name):
-            tile = held.tile([P, S], U32, name=name, align_bytes=64)
+            tile = shared.tile([P, S], U32, name=name, tag=name, align_bytes=64)
             nc.vector.tensor_copy(tile[:], window.bitcast(U32).indirect(offsets[:]))
             return tile
 
@@ -80,18 +85,18 @@ def tile_list_zoo_transfer_join_kernel(
             return tile
 
         idx2 = load_list(offs2, "idx2")
-        win2 = load_words(tab2_words[0], "win2", "B")
-        swin2 = load_scales(tab2_scales, "swin2", "C", nc.gpsimd)
-        w2_sraw = load_scales(w2_scales, "w2_sraw", "F", nc.vector)
+        win2 = load_words(tab2_words[0], "win2", "A")
+        swin2 = load_scales([tab2_scales], "swin2", "v2", nc.gpsimd)
         idx3 = load_list(offs3, "idx3")
         idx1 = load_list(offs, "idx1")
         p2 = load_list(pos2, "p2")
         p3 = load_list(pos3, "p3")
         p1 = load_list(pos1, "p1")
         w2_raw = load_packed(w2_words[0], "w2_raw")
-        swin3 = load_scales(tab3_scales, "swin3", "D", nc.vector)
-        w3_sraw = load_scales(w3_scales, "w3_sraw", "G", nc.vector)
-        swin1 = load_scales(tab_scales, "swin1", "E", nc.vector)
+        win3 = load_words(tab3_words[0], "win3", "B")
+        swin3 = load_scales([tab3_scales], "swin3", "D", nc.vector)
+        w23_sraw = load_scales([w2_scales, w3_scales], "w23_sraw", "C", nc.vector)
+        swin1 = load_scales([tab_scales], "swin1", "E", nc.vector)
 
         def load_margin(i):
             g, t = divmod(i, PACK)
@@ -110,9 +115,11 @@ def tile_list_zoo_transfer_join_kernel(
                 )
             return raw
 
-        def load_keep(c, slot):
-            tile = shared.tile([P, PACK, J], F32, name="keep%d" % c, tag=slot, align_bytes=64)
-            nc.sync.dma_start(tile[:], keep[PASS * c : PASS * (c + 1), :].rearrange("(p t) j -> p t j", t=PACK))
+        def load_keep(slot):
+            tile = shared.tile([P, 2, PACK, J], F32, name="keeps", tag=slot, align_bytes=64)
+            for c in range(2):
+                rows = keep[PASS * c : PASS * (c + 1), :].rearrange("(p t) j -> p t j", t=PACK)
+                nc.sync.dma_start(tile[:, c], rows)
             return tile
 
         def load_w4(g, slot):
@@ -123,81 +130,77 @@ def tile_list_zoo_transfer_join_kernel(
             return raw
 
         margins = [load_margin(i) for i in range(2 * PACK)]
-        w1_raw = [load_w1(0, "A")]
         w3_raw = load_packed(w3_words[0].rearrange("p n t -> p (n t)"), "w3_raw")
 
-        v2 = pick_words(win2[:], idx2, "v2")
-        win3 = load_words(tab3_words[0], "win3", "B")
         s2 = pick_scales(swin2, idx2, "s2")
+        v2 = pick_words(win2[:], idx2, "v2")
+        w1_raw = [load_w1(0, "A")]
+        w23_s = deal(w23_sraw, "w23_s")
         win1 = shared.tile([P, 2, T], I32, name="win1", tag="C", align_bytes=64)
         for a in range(2):
             nc.sync.dma_start(win1[:, a, :], tab_words[a].rearrange("p n t -> p (n t)").bitcast(I32))
-        w2 = deal(w2_raw, "w2")
-        w2_s = deal(w2_sraw, "w2_s")
         v3 = pick_words(win3[:], idx3, "v3")
         w1_raw.append(load_w1(1, "B"))
         s3 = pick_scales(swin3, idx3, "s3")
-        w4_raw = {1: load_w4(1, "D")}
+        w2 = deal(w2_raw, "w2")
         w3 = deal(w3_raw, "w3")
-        w3_s = deal(w3_sraw, "w3_s")
         s1 = pick_scales(swin1, idx1, "s1")
         v1 = [pick_words(win1[:, a, :], idx1, "v1_%d" % a) for a in range(2)]
-        keeps = [load_keep(0, "G"), load_keep(1, "E")]
+        w4_raw = {1: load_w4(1, "D")}
+        keeps = load_keep("E")
 
-        NB, NA = 4, 4
-        b_rows = [held.tile([P, S], F32, name="b_rows%d" % i) for i in range(NB)]
-        d_rows = [held.tile([P, S], F32, name="d_rows%d" % i) for i in range(NB)]
+        NB, NA = 4, 3
+        bd_rows = [held.tile([P, 2, S], F32, name="bd_rows%d" % i) for i in range(NB)]
         a_rows = [held.tile([P, S], F32, name="a_rows%d" % i) for i in range(NA)]
-        w1_q = [held.tile([P, 2, P], U32, name="w1_q%d" % i, align_bytes=64) for i in range(8)]
-        w1_s = [held.tile([P, 2, P], U8, name="w1_s%d" % i, align_bytes=64) for i in range(8)]
+        w1_q = [held.tile([P, PASS], U32, name="w1_q%d" % k, align_bytes=64) for k in range(4)]
+        w1_s = [held.tile([P, PASS], U8, name="w1_s%d" % k, align_bytes=64) for k in range(4)]
 
         def quantize(codes, scales, stage):
             nc.vector.quantize_mx(out=codes.bitcast(FP8X4), scales=scales, in_=stage)
 
-        def make_w1(i):
-            g, t = divmod(i, PACK)
-            stage = rounded.tile([P, 2 * PASS], BF16, name="w1_bf%d" % i, tag="w1_bf", align_bytes=64)
-            nc.scalar.copy(
-                stage[:].rearrange("p (a u e j) -> p a u j e", a=2, e=4, j=PACK),
-                w1_raw[g][:].rearrange("p a j (u t e) -> p t a u j e", t=PACK, e=4)[:, t],
-            )
-            quantize(w1_q[i][:].rearrange("p a m -> p (a m)"), w1_s[i][:].rearrange("p a m -> p (a m)"), stage[:])
+        def make_w1(k):
+            stage = rounded.tile([P, 2, 2 * PASS], BF16, name="w1_bf%d" % k, tag="rounded", align_bytes=64)
+            for n in range(2):
+                g, t = divmod(2 * k + n, PACK)
+                nc.scalar.copy(
+                    stage[:, n, :].rearrange("p (a u e j) -> p a u j e", a=2, e=4, j=PACK),
+                    w1_raw[g][:].rearrange("p a j (u t e) -> p t a u j e", t=PACK, e=4)[:, t],
+                )
+            quantize(w1_q[k][:], w1_s[k][:], stage[:].rearrange("p n x -> p (n x)"))
 
-        def make_b(i):
-            for h in range(2):
-                cols = slice(BANK * h, BANK * (h + 1))
+        def make_bd(i):
+            half = BANK // 2
+            for q in range(4):
+                cols = slice(half * q, half * (q + 1))
                 nc.tensor.matmul_mx(
-                    out=banks[h][:], lhsT=w2[:, 2 * P * i : 2 * P * (i + 1)].bitcast(FP4X4),
-                    lhsT_scale=w2_s[:, P * i : P * (i + 1)], rhs=v2[:, cols].bitcast(FP8X4), rhs_scale=s2[:, cols],
+                    out=banks[q][:, :half], lhsT=w2[:, 2 * P * i : 2 * P * (i + 1)].bitcast(FP4X4),
+                    lhsT_scale=w23_s[:, P * i : P * (i + 1)], rhs=v2[:, cols].bitcast(FP8X4), rhs_scale=s2[:, cols],
                     start=True, stop=True,
                 )
-                nc.scalar.copy(b_rows[i % NB][:, cols], banks[h][:])
-
-        def make_d(i):
-            for h in range(2):
-                cols = slice(BANK * h, BANK * (h + 1))
                 nc.tensor.matmul_mx(
-                    out=banks[2 + h][:], lhsT=w3[:, 4 * P * i : 4 * P * (i + 1)].bitcast(FP8X4),
-                    lhsT_scale=w3_s[:, P * i : P * (i + 1)], rhs=v3[:, cols].bitcast(FP8X4), rhs_scale=s3[:, cols],
+                    out=banks[q][:, half:], lhsT=w3[:, 4 * P * i : 4 * P * (i + 1)].bitcast(FP8X4),
+                    lhsT_scale=w23_s[4:, P * i : P * (i + 1)], rhs=v3[:, cols].bitcast(FP8X4), rhs_scale=s3[:, cols],
                     start=True, stop=True,
                 )
-                nc.scalar.copy(d_rows[i % NB][:, cols], banks[2 + h][:])
+                nc.scalar.copy(bd_rows[i % NB][:, :, cols], banks[q][:].rearrange("p (w c) -> p w c", w=2))
 
         def make_a(i):
             for h in range(2):
                 cols = slice(BANK * h, BANK * (h + 1))
                 bank = banks[4 + 2 * (i % 2) + h]
                 for a in range(2):
+                    held_cols = slice(P * (2 * (i % 2) + a), P * (2 * (i % 2) + a + 1))
                     nc.tensor.matmul_mx(
-                        out=bank[:], lhsT=w1_q[i][:, a, :].bitcast(FP8X4), lhsT_scale=w1_s[i][:, a, :],
+                        out=bank[:], lhsT=w1_q[i // 2][:, held_cols].bitcast(FP8X4), lhsT_scale=w1_s[i // 2][:, held_cols],
                         rhs=v1[a][:, cols].bitcast(FP8X4), rhs_scale=s1[4 * a :, cols],
                         start=(a == 0), stop=(a == 1),
                     )
                 nc.scalar.copy(a_rows[i % NA][:, cols], bank[:])
 
-        low = held.tile([P, PACK, J], F32, name="low")
         joined = shared.tile([P, 2, PACK, J], F32, name="joined", tag="C", align_bytes=64)
-        zoo, crate = joined[:, 0], joined[:, 1]
+        later = held.tile([P, 2, PACK, J], F32, name="later")
+        low = [joined[:, 0], later[:, 0]]
+        crate = [joined[:, 1], later[:, 1]]
         z_q = [held.tile([P, J], U32, name="z_q%d" % g, align_bytes=64) for g in range(2)]
         z_s = [held.tile([P, J], U8, name="z_s%d" % g, align_bytes=64) for g in range(2)]
         w4_q = [[held.tile([P, PASS], U32, name="w4_q%d%d" % (g, c), align_bytes=64) for c in range(2)] for g in range(2)]
@@ -206,21 +209,27 @@ def tile_list_zoo_transfer_join_kernel(
         def join(i):
             g, t = divmod(i, PACK)
             animal = picks.tile([P, J], F32, name="animal%d" % i, tag="animal")
-            nc.vector.tensor_copy(zoo[:, t, :], b_rows[i % NB][:].indirect(p2[:]))
             nc.vector.tensor_copy(animal[:], a_rows[i % NA][:].indirect(p1[:]))
-            nc.vector.tensor_copy(crate[:, t, :], d_rows[i % NB][:].indirect(p3[:]))
+            nc.vector.tensor_copy(low[g][:, t, :], bd_rows[i % NB][:, 0, :].indirect(p2[:]))
+            nc.vector.tensor_copy(crate[g][:, t, :], bd_rows[i % NB][:, 1, :].indirect(p3[:]))
             nc.vector.scalar_tensor_tensor(
-                out=low[:, t, :], in0=animal[:], scalar=margins[i][:], in1=zoo[:, t, :], op0=ALU.add, op1=ALU.min
+                out=low[g][:, t, :], in0=animal[:], scalar=margins[i][:], in1=low[g][:, t, :], op0=ALU.add, op1=ALU.min
             )
+            if g == 0:
+                nc.gpsimd.tensor_tensor(out=low[g][:, t, :], in0=low[g][:, t, :], in1=crate[g][:, t, :], op=ALU.mult)
 
         def make_z(g):
             stage = rounded.tile([P, J * PACK], BF16, name="z_bf%d" % g, tag="rounded", align_bytes=64)
-            nc.vector.tensor_tensor(
-                out=stage[:].rearrange("p (c i t) -> p c t i", i=4, t=PACK),
-                in0=low[:].rearrange("p t (c i) -> p c t i", i=4),
-                in1=crate.rearrange("p t (c i) -> p c t i", i=4),
-                op=ALU.mult,
-            )
+            dealt = stage[:].rearrange("p (c i t) -> p c t i", i=4, t=PACK)
+            if g == 0:
+                nc.scalar.copy(dealt, low[g].rearrange("p t (c i) -> p c t i", i=4))
+            else:
+                nc.vector.tensor_tensor(
+                    out=dealt,
+                    in0=low[g].rearrange("p t (c i) -> p c t i", i=4),
+                    in1=crate[g].rearrange("p t (c i) -> p c t i", i=4),
+                    op=ALU.mult,
+                )
             quantize(z_q[g][:], z_s[g][:], stage[:])
 
         def make_w4(g, c):
@@ -232,27 +241,26 @@ def tile_list_zoo_transfer_join_kernel(
             quantize(w4_q[g][c][:], w4_s[g][c][:], stage[:])
 
         AHEAD = 2
+        for k in range(2):
+            make_w1(k)
         for i in range(AHEAD):
-            make_b(i)
-            make_d(i)
-        for i in range(PACK):
-            make_w1(i)
+            make_bd(i)
         w4_raw[0] = load_w4(0, "A")
         for i in range(AHEAD):
             make_a(i)
         for i in range(8):
             ahead = i + AHEAD
             if ahead < 8:
-                if ahead + AHEAD < 8:
-                    make_w1(ahead + AHEAD)
-                make_b(ahead)
-                make_d(ahead)
+                if ahead in (2, 4):
+                    make_w1(ahead // 2 + 1)
                 make_a(ahead)
+                make_bd(ahead)
+            if i == 5:
+                make_z(0)
             if i >= 5:
                 make_w4(*divmod(i - 5, 2))
             join(i)
-            if i % PACK == PACK - 1:
-                make_z(i // PACK)
+        make_z(1)
         make_w4(1, 1)
 
         for g in range(2):
@@ -268,7 +276,7 @@ def tile_list_zoo_transfer_join_kernel(
             y = shared.tile([P, PACK, J], F32, name="y%d" % c, tag="BA"[c], align_bytes=64)
             rows = out_0[PASS * c : PASS * (c + 1), :].rearrange("(p t) j -> p t j", t=PACK)
             for t in range(PACK):
-                nc.vector.tensor_tensor(out=y[:, t, :], in0=banks[PACK * c + t][:], in1=keeps[c][:, t, :], op=ALU.mult)
+                nc.vector.tensor_tensor(out=y[:, t, :], in0=banks[PACK * c + t][:], in1=keeps[:, c, t, :], op=ALU.mult)
                 if t % 2 == 1:
                     nc.sync.dma_start(rows[:, t - 1 : t + 1, :], y[:, t - 1 : t + 1, :])
             stage = rounded.tile([P, J * PACK], BF16, name="y_bf%d" % c, tag="rounded", align_bytes=64)
@@ -277,7 +285,8 @@ def tile_list_zoo_transfer_join_kernel(
             if c == 0:
                 nc.scalar.copy(dealt, source)
             else:
-                nc.vector.tensor_copy(dealt, source)
+                nc.scalar.copy(dealt[:, :SCALAR_SHARE], source[:, :SCALAR_SHARE])
+                nc.vector.tensor_copy(dealt[:, SCALAR_SHARE:], source[:, SCALAR_SHARE:])
             y_q = held.tile([P, J], U32, name="y_q%d" % c, align_bytes=64)
             quantize(y_q[:], y_s[:, c, :], stage[:])
             nc.sync.dma_start(out_1[c].rearrange("p n t -> p (n t)").bitcast(I32), y_q[:].bitcast(I32))

@@ -20,7 +20,6 @@ PACK = 4
 PASS = P * PACK
 BANK = 512
 QUADS = 4
-SCALAR_SHARE = 40
 
 
 def tile_list_zoo_transfer_join_kernel(
@@ -38,6 +37,13 @@ def tile_list_zoo_transfer_join_kernel(
 
         banks = [psum.tile([P, BANK], F32, name="bank%d" % i) for i in range(8)]
 
+        taken = []
+
+        def take_banks(count):
+            first = len(taken)
+            taken.extend(banks[n % len(banks)] for n in range(first, first + count))
+            return taken[first:]
+
         def load_list(src, name):
             tile = lists.tile([P, src.shape[1]], U16, name=name)
             nc.sync.dma_start(tile[:], src)
@@ -48,18 +54,17 @@ def tile_list_zoo_transfer_join_kernel(
             nc.sync.dma_start(tile[:], src.rearrange("p n t -> p (n t)").bitcast(I32))
             return tile
 
-        def load_scales(sources, name, slot, zero_on):
-            tile = shared.tile([P, sources[0].shape[2]], U8, name=name, tag=slot, align_bytes=64)
-            zero_on.memset(tile[:].bitcast(I32), 0)
-            first = 0
-            for src in sources:
-                passes = src.shape[0]
-                for q in range(QUADS):
-                    rows = src[:, 4 * q : 4 * q + 4, :] if passes > 1 else src[0, 4 * q : 4 * q + 4, :]
-                    start = 32 * q + first
-                    nc.scalar.dma_start(tile[start : start + 4 * passes, :].bitcast(I32), rows.bitcast(I32))
-                first += 4 * passes
+        def zeroed_plane(width, name, slot, engine):
+            tile = shared.tile([P, width], U8, name=name, tag=slot, align_bytes=64)
+            engine.memset(tile[:].bitcast(I32), 0)
             return tile
+
+        def load_scales(tile, src, first=0, queue=nc.sync):
+            passes = src.shape[0]
+            for q in range(QUADS):
+                rows = src[:, 4 * q : 4 * q + 4, :] if passes > 1 else src[0, 4 * q : 4 * q + 4, :]
+                start = 32 * q + first
+                queue.dma_start(tile[start : start + 4 * passes, :].bitcast(I32), rows.bitcast(I32))
 
         def pick_words(window, offsets, name):
             tile = shared.tile([P, S], U32, name=name, tag=name, align_bytes=64)
@@ -79,41 +84,22 @@ def tile_list_zoo_transfer_join_kernel(
             )
             return tile
 
-        def load_packed(src, name):
-            tile = held.tile([P, src.shape[1]], U8, name=name, align_bytes=64)
+        def load_packed(src, name, slot):
+            tile = shared.tile([P, src.shape[1]], U8, name=name, tag=slot, align_bytes=64)
             nc.sync.dma_start(tile[:].bitcast(I32), src.bitcast(I32))
             return tile
 
-        idx2 = load_list(offs2, "idx2")
-        win2 = load_words(tab2_words[0], "win2", "A")
-        swin2 = load_scales([tab2_scales], "swin2", "v2", nc.gpsimd)
-        idx3 = load_list(offs3, "idx3")
-        idx1 = load_list(offs, "idx1")
-        p2 = load_list(pos2, "p2")
-        p3 = load_list(pos3, "p3")
-        p1 = load_list(pos1, "p1")
-        w2_raw = load_packed(w2_words[0], "w2_raw")
-        win3 = load_words(tab3_words[0], "win3", "B")
-        swin3 = load_scales([tab3_scales], "swin3", "D", nc.vector)
-        w23_sraw = load_scales([w2_scales, w3_scales], "w23_sraw", "C", nc.vector)
-        swin1 = load_scales([tab_scales], "swin1", "E", nc.vector)
+        def load_margins():
+            tile = held.tile([P, 2 * PACK, 8], F32, name="margins")
+            dealt = margin.rearrange("(g u t e o) -> g t u e o", g=2, t=PACK, e=4, o=1)
+            for i in range(2 * PACK):
+                with nc.allow_non_contiguous_dma(reason="one margin value a partition"):
+                    nc.gpsimd.dma_start(tile[:, i, 0:1], dealt[i // PACK, i % PACK])
+            return tile
 
-        def load_margin(i):
-            g, t = divmod(i, PACK)
-            col = held.tile([P, 1], F32, name="margin%d" % i)
-            dealt = margin[PASS * g : PASS * (g + 1)].rearrange("(u t e o) -> t u e o", t=PACK, e=4, o=1)
-            with nc.allow_non_contiguous_dma(reason="one margin value a partition"):
-                nc.gpsimd.dma_start(col[:], dealt[t])
-            return col
-
-        def load_w1(g, slot):
-            raw = shared.tile([P, 2, PACK, PASS], F32, name="w1_raw%d" % g, tag=slot, align_bytes=64)
-            for a in range(2):
-                nc.sync.dma_start(
-                    raw[:, a, :, :],
-                    w1[PASS * a : PASS * (a + 1), PASS * g : PASS * (g + 1)].rearrange("(p j) c -> p j c", j=PACK),
-                )
-            return raw
+        def load_w1(raw, g, a):
+            rows = w1[PASS * a : PASS * (a + 1), PASS * g : PASS * (g + 1)]
+            nc.sync.dma_start(raw[:, a, :, :], rows.rearrange("(p j) c -> p j c", j=PACK))
 
         def load_keep(slot):
             tile = shared.tile([P, 2, PACK, J], F32, name="keeps", tag=slot, align_bytes=64)
@@ -129,27 +115,47 @@ def tile_list_zoo_transfer_join_kernel(
                 nc.sync.dma_start(raw[:, t, :], rows[t])
             return raw
 
-        margins = [load_margin(i) for i in range(2 * PACK)]
-        w3_raw = load_packed(w3_words[0].rearrange("p n t -> p (n t)"), "w3_raw")
+        swin2 = zeroed_plane(T, "swin2", "v2", nc.vector)
+        swin3 = zeroed_plane(T, "swin3", "swin3", nc.vector)
+        swin1 = zeroed_plane(T, "swin1", "swin1", nc.vector)
+        w23_sraw = zeroed_plane(H, "w23_sraw", "w23_sraw", nc.gpsimd)
+        w1_raw = [shared.tile([P, 2, PACK, PASS], F32, name="w1_raw%d" % g, tag="EF"[g], align_bytes=64) for g in range(2)]
+
+        idx2 = load_list(offs2, "idx2")
+        load_scales(swin2, tab2_scales, queue=nc.scalar)
+        win2 = load_words(tab2_words[0], "win2", "A")
+        idx3 = load_list(offs3, "idx3")
+        win3 = load_words(tab3_words[0], "win3", "B")
+        load_scales(swin3, tab3_scales)
+        w2_raw = load_packed(w2_words[0], "w2_raw", "w2_raw")
+        w3_raw = load_packed(w3_words[0].rearrange("p n t -> p (n t)"), "w3_raw", "w3_raw")
+        load_w1(w1_raw[0], 0, 0)
+        idx1 = load_list(offs, "idx1")
+        load_scales(w23_sraw, w2_scales)
+        load_w1(w1_raw[0], 0, 1)
+        load_scales(w23_sraw, w3_scales, first=4)
+        load_scales(swin1, tab_scales)
+        win1 = [load_words(tab_words[a], "win1_%d" % a, "CD"[a]) for a in range(2)]
+        p2 = load_list(pos2, "p2")
+        p3 = load_list(pos3, "p3")
+        p1 = load_list(pos1, "p1")
+        for a in range(2):
+            load_w1(w1_raw[1], 1, a)
+        margins = load_margins()
 
         s2 = pick_scales(swin2, idx2, "s2")
         v2 = pick_words(win2[:], idx2, "v2")
-        w1_raw = [load_w1(0, "A")]
-        w23_s = deal(w23_sraw, "w23_s")
-        win1 = shared.tile([P, 2, T], I32, name="win1", tag="C", align_bytes=64)
-        for a in range(2):
-            nc.sync.dma_start(win1[:, a, :], tab_words[a].rearrange("p n t -> p (n t)").bitcast(I32))
         v3 = pick_words(win3[:], idx3, "v3")
-        w1_raw.append(load_w1(1, "B"))
         s3 = pick_scales(swin3, idx3, "s3")
+        s1 = pick_scales(swin1, idx1, "s1")
         w2 = deal(w2_raw, "w2")
         w3 = deal(w3_raw, "w3")
-        s1 = pick_scales(swin1, idx1, "s1")
-        v1 = [pick_words(win1[:, a, :], idx1, "v1_%d" % a) for a in range(2)]
-        w4_raw = {1: load_w4(1, "D")}
-        keeps = load_keep("E")
+        w23_s = deal(w23_sraw, "w23_s")
+        v1 = [pick_words(win1[a][:], idx1, "v1_%d" % a) for a in range(2)]
+        w4_raw = {1: load_w4(1, "C")}
+        keeps = load_keep("B")
 
-        NB, NA = 4, 3
+        NB, NA = 4, 4
         bd_rows = [held.tile([P, 2, S], F32, name="bd_rows%d" % i) for i in range(NB)]
         a_rows = [held.tile([P, S], F32, name="a_rows%d" % i) for i in range(NA)]
         w1_q = [held.tile([P, PASS], U32, name="w1_q%d" % k, align_bytes=64) for k in range(4)]
@@ -170,24 +176,23 @@ def tile_list_zoo_transfer_join_kernel(
 
         def make_bd(i):
             half = BANK // 2
-            for q in range(4):
+            for q, bank in enumerate(take_banks(4)):
                 cols = slice(half * q, half * (q + 1))
                 nc.tensor.matmul_mx(
-                    out=banks[q][:, :half], lhsT=w2[:, 2 * P * i : 2 * P * (i + 1)].bitcast(FP4X4),
+                    out=bank[:, :half], lhsT=w2[:, 2 * P * i : 2 * P * (i + 1)].bitcast(FP4X4),
                     lhsT_scale=w23_s[:, P * i : P * (i + 1)], rhs=v2[:, cols].bitcast(FP8X4), rhs_scale=s2[:, cols],
                     start=True, stop=True,
                 )
                 nc.tensor.matmul_mx(
-                    out=banks[q][:, half:], lhsT=w3[:, 4 * P * i : 4 * P * (i + 1)].bitcast(FP8X4),
+                    out=bank[:, half:], lhsT=w3[:, 4 * P * i : 4 * P * (i + 1)].bitcast(FP8X4),
                     lhsT_scale=w23_s[4:, P * i : P * (i + 1)], rhs=v3[:, cols].bitcast(FP8X4), rhs_scale=s3[:, cols],
                     start=True, stop=True,
                 )
-                nc.scalar.copy(bd_rows[i % NB][:, :, cols], banks[q][:].rearrange("p (w c) -> p w c", w=2))
+                nc.scalar.copy(bd_rows[i % NB][:, :, cols], bank[:].rearrange("p (w c) -> p w c", w=2))
 
         def make_a(i):
-            for h in range(2):
+            for h, bank in enumerate(take_banks(2)):
                 cols = slice(BANK * h, BANK * (h + 1))
-                bank = banks[4 + 2 * (i % 2) + h]
                 for a in range(2):
                     held_cols = slice(P * (2 * (i % 2) + a), P * (2 * (i % 2) + a + 1))
                     nc.tensor.matmul_mx(
@@ -197,8 +202,8 @@ def tile_list_zoo_transfer_join_kernel(
                     )
                 nc.scalar.copy(a_rows[i % NA][:, cols], bank[:])
 
-        joined = shared.tile([P, 2, PACK, J], F32, name="joined", tag="C", align_bytes=64)
-        later = held.tile([P, 2, PACK, J], F32, name="later")
+        joined = shared.tile([P, 2, PACK, J], F32, name="joined", tag="D", align_bytes=64)
+        later = shared.tile([P, 2, PACK, J], F32, name="later", tag="A", align_bytes=64)
         low = [joined[:, 0], later[:, 0]]
         crate = [joined[:, 1], later[:, 1]]
         z_q = [held.tile([P, J], U32, name="z_q%d" % g, align_bytes=64) for g in range(2)]
@@ -213,7 +218,7 @@ def tile_list_zoo_transfer_join_kernel(
             nc.vector.tensor_copy(low[g][:, t, :], bd_rows[i % NB][:, 0, :].indirect(p2[:]))
             nc.vector.tensor_copy(crate[g][:, t, :], bd_rows[i % NB][:, 1, :].indirect(p3[:]))
             nc.vector.scalar_tensor_tensor(
-                out=low[g][:, t, :], in0=animal[:], scalar=margins[i][:], in1=low[g][:, t, :], op0=ALU.add, op1=ALU.min
+                out=low[g][:, t, :], in0=animal[:], scalar=margins[:, i, 0:1], in1=low[g][:, t, :], op0=ALU.add, op1=ALU.min
             )
             if g == 0:
                 nc.gpsimd.tensor_tensor(out=low[g][:, t, :], in0=low[g][:, t, :], in1=crate[g][:, t, :], op=ALU.mult)
@@ -245,7 +250,7 @@ def tile_list_zoo_transfer_join_kernel(
             make_w1(k)
         for i in range(AHEAD):
             make_bd(i)
-        w4_raw[0] = load_w4(0, "A")
+        w4_raw[0] = load_w4(0, "E")
         for i in range(AHEAD):
             make_a(i)
         for i in range(8):
@@ -263,32 +268,36 @@ def tile_list_zoo_transfer_join_kernel(
         make_z(1)
         make_w4(1, 1)
 
+        ON_GPSIMD = (0, 4)
+        order = (0, 1, 4, 2, 3, 5, 6, 7)
         for g in range(2):
-            for i in range(8):
+            for i in order:
                 c, t = divmod(i, PACK)
                 cols = slice(P * t, P * (t + 1))
                 nc.tensor.matmul_mx(
                     out=banks[i][:], lhsT=w4_q[g][c][:, cols].bitcast(FP8X4), lhsT_scale=w4_s[g][c][:, cols],
                     rhs=z_q[g][:].bitcast(FP8X4), rhs_scale=z_s[g][:], start=(g == 0), stop=(g == 1),
                 )
+        y = [shared.tile([P, PACK, J], F32, name="y%d" % c, tag="FE"[c], align_bytes=64) for c in range(2)]
+        for i in order:
+            c, t = divmod(i, PACK)
+            if i in ON_GPSIMD:
+                nc.scalar.copy(y[c][:, t, :], banks[i][:])
+                nc.gpsimd.tensor_tensor(out=y[c][:, t, :], in0=y[c][:, t, :], in1=keeps[:, c, t, :], op=ALU.mult)
+            else:
+                nc.vector.tensor_tensor(out=y[c][:, t, :], in0=banks[i][:], in1=keeps[:, c, t, :], op=ALU.mult)
+            if t % 2 == 1:
+                rows = out_0[PASS * c : PASS * (c + 1), :].rearrange("(p t) j -> p t j", t=PACK)
+                nc.sync.dma_start(rows[:, t - 1 : t + 1, :], y[c][:, t - 1 : t + 1, :])
+        y_bf = []
+        for c, copy in enumerate((nc.scalar.copy, nc.vector.tensor_copy)):
+            stage = rounded.tile([P, J * PACK], BF16, name="y_bf%d" % c, tag="rounded", align_bytes=64)
+            copy(stage[:].rearrange("p (c i t) -> p c t i", i=4, t=PACK), y[c][:].rearrange("p t (c i) -> p c t i", i=4))
+            y_bf.append(stage)
         y_s = held.tile([P, 2, J], U8, name="y_s", align_bytes=64)
         for c in range(2):
-            y = shared.tile([P, PACK, J], F32, name="y%d" % c, tag="BA"[c], align_bytes=64)
-            rows = out_0[PASS * c : PASS * (c + 1), :].rearrange("(p t) j -> p t j", t=PACK)
-            for t in range(PACK):
-                nc.vector.tensor_tensor(out=y[:, t, :], in0=banks[PACK * c + t][:], in1=keeps[:, c, t, :], op=ALU.mult)
-                if t % 2 == 1:
-                    nc.sync.dma_start(rows[:, t - 1 : t + 1, :], y[:, t - 1 : t + 1, :])
-            stage = rounded.tile([P, J * PACK], BF16, name="y_bf%d" % c, tag="rounded", align_bytes=64)
-            dealt = stage[:].rearrange("p (c i t) -> p c t i", i=4, t=PACK)
-            source = y[:].rearrange("p t (c i) -> p c t i", i=4)
-            if c == 0:
-                nc.scalar.copy(dealt, source)
-            else:
-                nc.scalar.copy(dealt[:, :SCALAR_SHARE], source[:, :SCALAR_SHARE])
-                nc.vector.tensor_copy(dealt[:, SCALAR_SHARE:], source[:, SCALAR_SHARE:])
             y_q = held.tile([P, J], U32, name="y_q%d" % c, align_bytes=64)
-            quantize(y_q[:], y_s[:, c, :], stage[:])
+            quantize(y_q[:], y_s[:, c, :], y_bf[c][:])
             nc.sync.dma_start(out_1[c].rearrange("p n t -> p (n t)").bitcast(I32), y_q[:].bitcast(I32))
         for q in range(QUADS):
             queue = nc.sync if q % 2 == 0 else nc.scalar

from contextlib import ExitStack

import concourse.mybir as mybir

K, K2, T, S, J, H, N = 1024, 512, 2048, 1024, 512, 1024, 1024
FLOPS = 2 * S * H * (K + 2 * K2) + 2 * J * H * N

F32 = mybir.dt.float32
BF16 = mybir.dt.bfloat16
I32 = mybir.dt.int32
U32 = mybir.dt.uint32
U16 = mybir.dt.uint16
U8 = mybir.dt.uint8
FP8X4 = mybir.dt.float8_e4m3fn_x4
FP4X4 = mybir.dt.float4_e2m1fn_x4
ALU = mybir.AluOpType

P = 128
PACK = 4
PASS = P * PACK
BANK = 512
QUADS = 4


def tile_list_zoo_transfer_join_kernel(
    tc, tab_words, tab_scales, tab2_words, tab2_scales, tab3_words, tab3_scales, offs, offs2, offs3,
    pos1, pos2, pos3, w1, w2_words, w2_scales, w3_words, w3_scales, margin, w4, keep, out_0, out_1, out_2,
):
    nc = tc.nc
    with ExitStack() as ctx:
        lists = ctx.enter_context(tc.tile_pool(name="lists", bufs=1))
        held = ctx.enter_context(tc.tile_pool(name="held", bufs=1))
        shared = ctx.enter_context(tc.tile_pool(name="shared", bufs=1))
        rounded = ctx.enter_context(tc.tile_pool(name="rounded", bufs=5))
        picks = ctx.enter_context(tc.tile_pool(name="picks", bufs=2))
        psum = ctx.enter_context(tc.psum_pool(name="psum", bufs=1))

        banks = [psum.tile([P, BANK], F32, name="bank%d" % i) for i in range(8)]

        taken = []

        def take_banks(count):
            first = len(taken)
            taken.extend(banks[n % len(banks)] for n in range(first, first + count))
            return taken[first:]

        def load_list(src, name):
            tile = lists.tile([P, src.shape[1]], U16, name=name)
            nc.sync.dma_start(tile[:], src)
            return tile

        def load_words(src, name, slot):
            tile = shared.tile([P, T], I32, name=name, tag=slot, align_bytes=64)
            nc.sync.dma_start(tile[:], src.rearrange("p n t -> p (n t)").bitcast(I32))
            return tile

        def zeroed_plane(width, name, slot, engine):
            tile = shared.tile([P, width], U8, name=name, tag=slot, align_bytes=64)
            engine.memset(tile[:].bitcast(I32), 0)
            return tile

        def load_scales(tile, src, first=0, queue=nc.sync):
            passes = src.shape[0]
            for q in range(QUADS):
                rows = src[:, 4 * q : 4 * q + 4, :] if passes > 1 else src[0, 4 * q : 4 * q + 4, :]
                start = 32 * q + first
                queue.dma_start(tile[start : start + 4 * passes, :].bitcast(I32), rows.bitcast(I32))

        def pick_words(window, offsets, name):
            tile = shared.tile([P, S], U32, name=name, tag=name, align_bytes=64)
            nc.vector.tensor_copy(tile[:], window.bitcast(U32).indirect(offsets[:]))
            return tile

        def pick_scales(window, offsets, name):
            tile = held.tile([P, S], U8, name=name, align_bytes=64)
            nc.vector.tensor_copy(tile[:], window[:].indirect(offsets[:]))
            return tile

        def deal(raw, name):
            tile = held.tile([P, raw.shape[1]], U8, name=name, align_bytes=64)
            nc.vector.tensor_copy(
                tile[:].bitcast(I32).rearrange("p (g t u w) -> p g t u w", g=2, t=PACK, u=32),
                raw[:].bitcast(I32).rearrange("p (g u t w) -> p g t u w", g=2, t=PACK, u=32),
            )
            return tile

        def load_packed(src, name, slot):
            tile = shared.tile([P, src.shape[1]], U8, name=name, tag=slot, align_bytes=64)
            nc.sync.dma_start(tile[:].bitcast(I32), src.bitcast(I32))
            return tile

        def load_margins():
            tile = held.tile([P, 2 * PACK, 8], F32, name="margins")
            dealt = margin.rearrange("(g u t e o) -> g t u e o", g=2, t=PACK, e=4, o=1)
            for i in range(2 * PACK):
                with nc.allow_non_contiguous_dma(reason="one margin value a partition"):
                    nc.gpsimd.dma_start(tile[:, i, 0:1], dealt[i // PACK, i % PACK])
            return tile

        def load_w1(raw, g, a):
            rows = w1[PASS * a : PASS * (a + 1), PASS * g : PASS * (g + 1)]
            nc.sync.dma_start(raw[:, a, :, :], rows.rearrange("(p j) c -> p j c", j=PACK))

        def load_keep(slot):
            tile = shared.tile([P, 2, PACK, J], F32, name="keeps", tag=slot, align_bytes=64)
            for c in range(2):
                rows = keep[PASS * c : PASS * (c + 1), :].rearrange("(p t) j -> p t j", t=PACK)
                nc.sync.dma_start(tile[:, c], rows)
            return tile

        def load_w4(g, slot):
            raw = shared.tile([P, PACK, N], F32, name="w4_raw%d" % g, tag=slot, align_bytes=64)
            rows = w4[PASS * g : PASS * (g + 1), :].rearrange("(u t e) n -> t u e n", t=PACK, e=4)
            for t in range(PACK):
                nc.sync.dma_start(raw[:, t, :], rows[t])
            return raw

        swin2 = zeroed_plane(T, "swin2", "v2", nc.vector)
        swin3 = zeroed_plane(T, "swin3", "swin3", nc.vector)
        swin1 = zeroed_plane(T, "swin1", "swin1", nc.vector)
        w23_sraw = zeroed_plane(H, "w23_sraw", "w23_sraw", nc.gpsimd)
        w1_raw = [shared.tile([P, 2, PACK, PASS], F32, name="w1_raw%d" % g, tag="EF"[g], align_bytes=64) for g in range(2)]

        idx2 = load_list(offs2, "idx2")
        load_scales(swin2, tab2_scales, queue=nc.scalar)
        win2 = load_words(tab2_words[0], "win2", "A")
        idx3 = load_list(offs3, "idx3")
        win3 = load_words(tab3_words[0], "win3", "B")
        load_scales(swin3, tab3_scales)
        w2_raw = load_packed(w2_words[0], "w2_raw", "w2_raw")
        w3_raw = load_packed(w3_words[0].rearrange("p n t -> p (n t)"), "w3_raw", "w3_raw")
        load_w1(w1_raw[0], 0, 0)
        idx1 = load_list(offs, "idx1")
        load_scales(w23_sraw, w2_scales)
        load_w1(w1_raw[0], 0, 1)
        load_scales(w23_sraw, w3_scales, first=4)
        load_scales(swin1, tab_scales)
        win1 = [load_words(tab_words[a], "win1_%d" % a, "CD"[a]) for a in range(2)]
        p2 = load_list(pos2, "p2")
        p3 = load_list(pos3, "p3")
        p1 = load_list(pos1, "p1")
        for a in range(2):
            load_w1(w1_raw[1], 1, a)
        margins = load_margins()

        s2 = pick_scales(swin2, idx2, "s2")
        v2 = pick_words(win2[:], idx2, "v2")
        v3 = pick_words(win3[:], idx3, "v3")
        s3 = pick_scales(swin3, idx3, "s3")
        s1 = pick_scales(swin1, idx1, "s1")
        w2 = deal(w2_raw, "w2")
        w3 = deal(w3_raw, "w3")
        w23_s = deal(w23_sraw, "w23_s")
        v1 = [pick_words(win1[a][:], idx1, "v1_%d" % a) for a in range(2)]
        w4_raw = {1: load_w4(1, "C")}
        keeps = load_keep("B")

        NB, NA = 4, 4
        bd_rows = [held.tile([P, 2, S], F32, name="bd_rows%d" % i) for i in range(NB)]
        a_rows = [held.tile([P, S], F32, name="a_rows%d" % i) for i in range(NA)]
        w1_q = [held.tile([P, PASS], U32, name="w1_q%d" % k, align_bytes=64) for k in range(4)]
        w1_s = [held.tile([P, PASS], U8, name="w1_s%d" % k, align_bytes=64) for k in range(4)]

        def quantize(codes, scales, stage):
            nc.vector.quantize_mx(out=codes.bitcast(FP8X4), scales=scales, in_=stage)

        def make_w1(k):
            stage = rounded.tile([P, 2, 2 * PASS], BF16, name="w1_bf%d" % k, tag="rounded", align_bytes=64)
            for n in range(2):
                g, t = divmod(2 * k + n, PACK)
                nc.scalar.copy(
                    stage[:, n, :].rearrange("p (a u e j) -> p a u j e", a=2, e=4, j=PACK),
                    w1_raw[g][:].rearrange("p a j (u t e) -> p t a u j e", t=PACK, e=4)[:, t],
                )
            quantize(w1_q[k][:], w1_s[k][:], stage[:].rearrange("p n x -> p (n x)"))

        def make_bd(i):
            half = BANK // 2
            for q, bank in enumerate(take_banks(4)):
                cols = slice(half * q, half * (q + 1))
                nc.tensor.matmul_mx(
                    out=bank[:, :half], lhsT=w2[:, 2 * P * i : 2 * P * (i + 1)].bitcast(FP4X4),
                    lhsT_scale=w23_s[:, P * i : P * (i + 1)], rhs=v2[:, cols].bitcast(FP8X4), rhs_scale=s2[:, cols],
                    start=True, stop=True,
                )
                nc.tensor.matmul_mx(
                    out=bank[:, half:], lhsT=w3[:, 4 * P * i : 4 * P * (i + 1)].bitcast(FP8X4),
                    lhsT_scale=w23_s[4:, P * i : P * (i + 1)], rhs=v3[:, cols].bitcast(FP8X4), rhs_scale=s3[:, cols],
                    start=True, stop=True,
                )
                nc.scalar.copy(bd_rows[i % NB][:, :, cols], bank[:].rearrange("p (w c) -> p w c", w=2))

        def make_a(i):
            for h, bank in enumerate(take_banks(2)):
                cols = slice(BANK * h, BANK * (h + 1))
                for a in range(2):
                    held_cols = slice(P * (2 * (i % 2) + a), P * (2 * (i % 2) + a + 1))
                    nc.tensor.matmul_mx(
                        out=bank[:], lhsT=w1_q[i // 2][:, held_cols].bitcast(FP8X4), lhsT_scale=w1_s[i // 2][:, held_cols],
                        rhs=v1[a][:, cols].bitcast(FP8X4), rhs_scale=s1[4 * a :, cols],
                        start=(a == 0), stop=(a == 1),
                    )
                nc.scalar.copy(a_rows[i % NA][:, cols], bank[:])

        joined = shared.tile([P, 2, PACK, J], F32, name="joined", tag="D", align_bytes=64)
        later = shared.tile([P, 2, PACK, J], F32, name="later", tag="A", align_bytes=64)
        low = [joined[:, 0], later[:, 0]]
        crate = [joined[:, 1], later[:, 1]]
        z_q = [held.tile([P, J], U32, name="z_q%d" % g, align_bytes=64) for g in range(2)]
        z_s = [held.tile([P, J], U8, name="z_s%d" % g, align_bytes=64) for g in range(2)]
        w4_q = [[held.tile([P, PASS], U32, name="w4_q%d%d" % (g, c), align_bytes=64) for c in range(2)] for g in range(2)]
        w4_s = [[held.tile([P, PASS], U8, name="w4_s%d%d" % (g, c), align_bytes=64) for c in range(2)] for g in range(2)]

        def join(i):
            g, t = divmod(i, PACK)
            animal = picks.tile([P, J], F32, name="animal%d" % i, tag="animal")
            nc.vector.tensor_copy(animal[:], a_rows[i % NA][:].indirect(p1[:]))
            nc.vector.tensor_copy(low[g][:, t, :], bd_rows[i % NB][:, 0, :].indirect(p2[:]))
            nc.vector.tensor_copy(crate[g][:, t, :], bd_rows[i % NB][:, 1, :].indirect(p3[:]))
            nc.vector.scalar_tensor_tensor(
                out=low[g][:, t, :], in0=animal[:], scalar=margins[:, i, 0:1], in1=low[g][:, t, :], op0=ALU.add, op1=ALU.min
            )
            if g == 0:
                nc.gpsimd.tensor_tensor(out=low[g][:, t, :], in0=low[g][:, t, :], in1=crate[g][:, t, :], op=ALU.mult)

        def make_z(g):
            stage = rounded.tile([P, J * PACK], BF16, name="z_bf%d" % g, tag="rounded", align_bytes=64)
            dealt = stage[:].rearrange("p (c i t) -> p c t i", i=4, t=PACK)
            if g == 0:
                nc.scalar.copy(dealt, low[g].rearrange("p t (c i) -> p c t i", i=4))
            else:
                nc.vector.tensor_tensor(
                    out=dealt,
                    in0=low[g].rearrange("p t (c i) -> p c t i", i=4),
                    in1=crate[g].rearrange("p t (c i) -> p c t i", i=4),
                    op=ALU.mult,
                )
            quantize(z_q[g][:], z_s[g][:], stage[:])

        def make_w4(g, c):
            stage = rounded.tile([P, PASS * PACK], BF16, name="w4_bf%d%d" % (g, c), tag="rounded", align_bytes=64)
            nc.scalar.copy(
                stage[:].rearrange("p (t m j) -> p m j t", t=PACK, j=PACK),
                w4_raw[g][:, :, PASS * c : PASS * (c + 1)].rearrange("p j (m t) -> p m j t", t=PACK),
            )
            quantize(w4_q[g][c][:], w4_s[g][c][:], stage[:])

        AHEAD = 2
        for k in range(2):
            make_w1(k)
        for i in range(AHEAD):
            make_bd(i)
        w4_raw[0] = load_w4(0, "E")
        for i in range(AHEAD):
            make_a(i)
        for i in range(8):
            ahead = i + AHEAD
            if ahead < 8:
                if ahead in (2, 4):
                    make_w1(ahead // 2 + 1)
                make_a(ahead)
                make_bd(ahead)
            if i == 5:
                make_z(0)
            if i >= 5:
                make_w4(*divmod(i - 5, 2))
            join(i)
        make_z(1)
        make_w4(1, 1)

        ON_GPSIMD = (0, 4)
        order = (0, 1, 4, 2, 3, 5, 6, 7)
        for g in range(2):
            for i in order:
                c, t = divmod(i, PACK)
                cols = slice(P * t, P * (t + 1))
                nc.tensor.matmul_mx(
                    out=banks[i][:], lhsT=w4_q[g][c][:, cols].bitcast(FP8X4), lhsT_scale=w4_s[g][c][:, cols],
                    rhs=z_q[g][:].bitcast(FP8X4), rhs_scale=z_s[g][:], start=(g == 0), stop=(g == 1),
                )
        y = [shared.tile([P, PACK, J], F32, name="y%d" % c, tag="FE"[c], align_bytes=64) for c in range(2)]
        for i in order:
            c, t = divmod(i, PACK)
            if i in ON_GPSIMD:
                nc.scalar.copy(y[c][:, t, :], banks[i][:])
                nc.gpsimd.tensor_tensor(out=y[c][:, t, :], in0=y[c][:, t, :], in1=keeps[:, c, t, :], op=ALU.mult)
            else:
                nc.vector.tensor_tensor(out=y[c][:, t, :], in0=banks[i][:], in1=keeps[:, c, t, :], op=ALU.mult)
            if t % 2 == 1:
                rows = out_0[PASS * c : PASS * (c + 1), :].rearrange("(p t) j -> p t j", t=PACK)
                nc.sync.dma_start(rows[:, t - 1 : t + 1, :], y[c][:, t - 1 : t + 1, :])
        y_bf = []
        for c, copy in enumerate((nc.scalar.copy, nc.vector.tensor_copy)):
            stage = rounded.tile([P, J * PACK], BF16, name="y_bf%d" % c, tag="rounded", align_bytes=64)
            copy(stage[:].rearrange("p (c i t) -> p c t i", i=4, t=PACK), y[c][:].rearrange("p t (c i) -> p c t i", i=4))
            y_bf.append(stage)
        y_s = held.tile([P, 2, J], U8, name="y_s", align_bytes=64)
        for c in range(2):
            y_q = held.tile([P, J], U32, name="y_q%d" % c, align_bytes=64)
            quantize(y_q[:], y_s[:, c, :], y_bf[c][:])
            nc.sync.dma_start(out_1[c].rearrange("p n t -> p (n t)").bitcast(I32), y_q[:].bitcast(I32))
        for q in range(QUADS):
            queue = nc.sync if q % 2 == 0 else nc.scalar
            queue.dma_start(
                out_2[:, 4 * q : 4 * q + 4, :].rearrange("g r j -> r g j").bitcast(I32),
                y_s[32 * q : 32 * q + 4, :, :].bitcast(I32),
            )
